import numpy as np
import ml_dtypes


def mxq(x, axis, fmt="e4m3"):
    dtype, down = {"e4m3": (ml_dtypes.float8_e4m3fn, 7), "e5m2": (ml_dtypes.float8_e5m2, 14)}[fmt]
    v = np.moveaxis(np.asarray(x, np.float32).astype(ml_dtypes.bfloat16).astype(np.float64), axis, -1)
    blocks = v.reshape(v.shape[:-1] + (-1, 32))
    amax = np.abs(blocks).max(-1, keepdims=True)
    byte = np.maximum(np.where(amax > 0, np.frexp(amax)[1] - 1 + 127, 0) - down, 1)
    scale = np.exp2(byte - 127.0)
    codes = (blocks / scale).astype(np.float32).astype(dtype).astype(np.float64)
    return np.moveaxis((codes * scale).reshape(v.shape), -1, axis)


WIDE = False


def mx_kscale(k):
    if not WIDE:
        return np.ones(k)
    levels = np.array([10, -10, 5, -5, 0])
    if k % 512:
        return np.exp2(np.random.permutation(np.resize(levels, k // 32))).repeat(32)
    a = np.empty((k // 512, 16))
    for p in range(k // 512):
        a[p, :8] = np.random.permutation(np.resize(levels, 8))
        for g in range(8):
            far = levels[np.abs(levels - a[p, g]) >= 10]
            a[p, g + 8] = far[np.random.randint(len(far))]
    return np.exp2(a.ravel()).repeat(32)


def f64(x):
    return np.asarray(x).astype(np.float64)


def striped(idx):
    return np.tile(np.asarray(idx).reshape(-1, 16).T, (8, 1)).astype(np.uint16)


def unstriped(offs):
    return offs[:16].T.reshape(-1).astype(np.int64)


E2M1 = np.array([0.0, 0.5, 1.0, 1.5, 2.0, 3.0, 4.0, 6.0, -0.0, -0.5, -1.0, -1.5, -2.0, -3.0, -4.0, -6.0])


def pack_weight(w, fmt):
    k, n = w.shape
    w = f64(np.asarray(w, np.float32).astype(ml_dtypes.bfloat16)).reshape(k // 32, 32, n)
    amax = np.abs(w).max(1)
    if fmt == "e4m3":
        byte = np.frexp(amax)[1] - 1 + 127 - 7
    else:
        mant, ex = np.frexp(amax / 6.0)
        byte = np.where(mant > 0.5, ex, ex - 1) + 127
    byte = np.clip(np.where(amax > 0, byte, 1), 1, 254)
    scaled = (w * np.exp2(127.0 - byte)[:, None, :]).reshape(k, n).astype(np.float32)
    by_word = np.ascontiguousarray(scaled.reshape(k // 512, 128, 4, n).transpose(0, 1, 3, 2))
    if fmt == "e4m3":
        words = by_word.astype(ml_dtypes.float8_e4m3fn).view(np.uint8)
    else:
        c = by_word.astype(ml_dtypes.float4_e2m1fn).view(np.uint8) & 0xF
        words = (c[..., 0::2] | (c[..., 1::2] << 4)).reshape(k // 512, 128, 2 * n)
    return np.ascontiguousarray(words), np.ascontiguousarray(byte.astype(np.uint8).reshape(k // 512, 16, n))


def unpack_weight(words, scales, fmt):
    g, _, n = scales.shape
    words = np.ascontiguousarray(words).reshape(g, 128, n, -1)
    if fmt == "e4m3":
        vals = words.view(ml_dtypes.float8_e4m3fn).astype(np.float64)
    else:
        nib = np.empty((g, 128, n, 4), np.uint8)
        nib[..., 0::2] = words & 0xF
        nib[..., 1::2] = words >> 4
        vals = E2M1[nib]
    vals = vals * np.repeat(np.exp2(scales.astype(np.float64) - 127.0), 8, axis=1)[..., None]
    return vals.transpose(0, 1, 3, 2).reshape(g * 512, n)


D, E, T, I, Q, G = 512, 512, 1024, 256, 512, 32


def setup_inputs():
    n = np.random.standard_normal
    idx = np.random.permutation(T)[:I]
    fd = mx_kscale(D)
    fq = mx_kscale(Q)
    keysp = pack_weight(n((D, T)) / fd[:, None], "e2m1")
    return {
        "query": (n((D, Q)) * 0.8 / np.sqrt(D) * fd[:, None]).astype(np.float32),
        "query2": (n((D, Q)) * 0.8 / np.sqrt(D) * fd[:, None]).astype(np.float32),
        "keys_words": keysp[0],
        "keys_scales": keysp[1],
        "qs": (np.random.uniform(2.0, 8.0, (Q, 1)) * fq[:, None]).astype(np.float32),
        "grows": (n((Q, E)) / fq[:, None]).astype(np.float32),
        "old": (n((E, T)) * 2.0).astype(np.float32),
        "fade": (np.random.uniform(0.5, 1.0, (1, T))).astype(np.float32),
        "offs": striped(idx),
    }


def reference(query, query2, keys_words, keys_scales, qs, grows, old, fade, offs):
    idx = unstriped(offs)
    keysu = unpack_weight(keys_words, keys_scales, "e2m1")
    queryq = mxq(f64(query), 0, "e4m3")
    keysidxg = keysu[:, idx]
    a = queryq.T @ keysidxg
    query2q = mxq(f64(query2), 0, "e4m3")
    b = query2q.T @ keysidxg
    pa = np.exp(a)
    sa = pa.reshape(Q, G, I // G).sum(axis=2)
    z = np.sum(sa, axis=1, keepdims=True)
    pb = np.exp(b)
    sb = pb.reshape(Q, G, I // G).sum(axis=2)
    r = sa / z / sb
    rr = np.repeat(r, I // G, axis=1)
    w = pb * rr
    wq = w * f64(qs)
    growsq = mxq(f64(grows), 0, "e4m3")
    wqq = mxq(wq, 0, "e4m3")
    gv = growsq.T @ wqq
    gf = np.zeros((E, T))
    gf[:, idx] = gv
    y = f64(old) * f64(fade) + gf
    return y

@@ -1,0 +1,258 @@
+from contextlib import ExitStack
+
+import concourse.mybir as mybir
+from concourse.masks import make_identity
+
+D, E, T, I, Q, G = 512, 512, 1024, 256, 512, 32
+FLOPS = 2 * (2 * D * Q * I + Q * E * I)
+
+F32 = mybir.dt.float32
+BF16 = mybir.dt.bfloat16
+I32 = mybir.dt.int32
+U32 = mybir.dt.uint32
+U16 = mybir.dt.uint16
+U8 = mybir.dt.uint8
+FP8X4 = mybir.dt.float8_e4m3fn_x4
+FP4X4 = mybir.dt.float4_e2m1fn_x4
+ALU = mybir.AluOpType
+ACT = mybir.ActivationFunctionType
+AX = mybir.AxisListType
+
+P = 128
+PACK = 4
+PAGE = I // G
+HALVES = 2
+HS = I // HALVES
+HG = G // HALVES
+BANK = 512
+GP_TILES = 2
+GP_COLS = 256
+Q2_VECTOR = 80
+Q1_VECTOR = 40
+V_COLS = 256
+VECTOR_COPIES = (0, 3)
+VECTOR_SCATTERS = (0,)
+
+
+def tile_attend_bpagethensecond_v_kernel(
+    tc, query, query2, keys_words, keys_scales, qs, grows, old, fade, offs, out
+):
+    nc = tc.nc
+    with ExitStack() as ctx:
+        sb = ctx.enter_context(tc.tile_pool(name="sb", bufs=1))
+        ps = ctx.enter_context(tc.psum_pool(name="ps", bufs=1))
+
+        offsets = sb.tile([P, I // 16], U16, name="offsets")
+        key_words = sb.tile([P, T], U16, name="key_words")
+        key_bytes = sb.tile([P, T], U8, name="key_bytes")
+        nc.gpsimd.memset(key_bytes[:].bitcast(I32), 0)
+
+        nc.sync.dma_start(offsets[:], offs)
+        fade_cols = sb.tile([P, 2, PACK], F32, name="fade_cols")
+        nc.sync.dma_start(fade_cols[:], fade.rearrange("o (h p c) -> p (o h) c", h=2, c=PACK))
+        nc.sync.dma_start(key_words[:].bitcast(I32), keys_words[0].bitcast(I32))
+        for u in range(4):
+            nc.sync.dma_start(
+                key_bytes[32 * u : 32 * u + 4, :].bitcast(I32), keys_scales[0, 4 * u : 4 * u + 4, :].bitcast(I32)
+            )
+        q2_raw = sb.tile([P, PACK, Q], F32, name="q2_raw")
+        nc.sync.dma_start(q2_raw[:], query2.rearrange("(p j) q -> p j q", j=PACK))
+        q1_raw = sb.tile([P, PACK, Q], F32, name="q1_raw")
+        nc.sync.dma_start(q1_raw[:], query.rearrange("(p j) q -> p j q", j=PACK))
+        row_scale = sb.tile([P, PACK], F32, name="row_scale")
+        nc.sync.dma_start(row_scale[:], qs.rearrange("(p j) o -> p (j o)", j=PACK))
+        old_t = [sb.tile([P, T], F32, name="old%d" % j) for j in range(4)]
+        g_raw = sb.tile([P, PACK, E], F32, name="g_raw")
+        for j in range(4):
+            if j == 1:
+                nc.sync.dma_start(g_raw[:], grows.rearrange("(p j) e -> p j e", j=PACK))
+            nc.sync.dma_start(old_t[j][:], old[j * P : (j + 1) * P, :])
+
+        ident = sb.tile([P, P], F32, name="ident")
+        make_identity(nc, ident[:])
+        gf = [sb.tile([P, T], F32, name="gf%d" % j) for j in range(4)]
+        for j in range(4):
+            (nc.vector if j < 4 else nc.gpsimd).memset(gf[j][:], 0.0)
+
+        kw = sb.tile([P, I], U16, name="kw", align_bytes=64)
+        kb = sb.tile([P, I], U8, name="kb", align_bytes=64)
+        nc.vector.tensor_copy(kw[:], key_words[:].indirect(offsets[:]))
+        nc.vector.tensor_copy(kb[:], key_bytes[:].indirect(offsets[:]))
+
+        def quantise(grouped, words, name):
+            codes = sb.tile([P, words], U32, name=name + "_codes", align_bytes=64)
+            scales = sb.tile([P, words], U8, name=name + "_scales", align_bytes=64)
+            nc.vector.quantize_mx(out=codes[:].bitcast(FP8X4), scales=scales[:], in_=grouped)
+            return codes, scales
+
+        def deal(raw, name, split):
+            grouped = sb.tile([P, PACK, P, PACK], BF16, name=name, align_bytes=64)
+            dst = grouped[:].rearrange("p r m j -> p m j r")
+            src = raw[:].rearrange("p j (m r) -> p m j r", r=PACK)
+            nc.vector.tensor_copy(dst[:, :split], src[:, :split])
+            nc.scalar.copy(dst[:, split:], src[:, split:])
+            return quantise(grouped[:].rearrange("p r m j -> p (r m j)"), Q, name)
+
+        def page_sums(tile, name, back_tag):
+            turned_ps = ps.tile([P, P], F32, name=name + "_turned_ps")
+            for k in range(PAGE):
+                nc.tensor.matmul(
+                    turned_ps[:],
+                    lhsT=tile[:, k, :],
+                    rhs=ident[:],
+                    is_transpose=True,
+                    start=(k == 0),
+                    stop=(k == PAGE - 1),
+                )
+            return turned_ps
+
+        q2c, q2s = deal(q2_raw, "q2", Q2_VECTOR)
+        b_ps = [ps.tile([P, PACK, HS], F32, name="b_ps%d" % h, tag="bg%d" % h) for h in range(HALVES)]
+        for h in range(HALVES):
+            for r in range(PACK):
+                nc.tensor.matmul_mx(
+                    b_ps[h][:, r, :],
+                    lhsT=q2c[:, r * P : (r + 1) * P].bitcast(FP8X4),
+                    lhsT_scale=q2s[:, r * P : (r + 1) * P],
+                    rhs=kw[:, h * HS : (h + 1) * HS].bitcast(FP4X4),
+                    rhs_scale=kb[:, h * HS : (h + 1) * HS],
+                    start=True,
+                    stop=True,
+                )
+
+        q1c, q1s = deal(q1_raw, "q1", Q1_VECTOR)
+        a_ps = [ps.tile([P, 2, I], F32, name="a_ps%d" % u, tag="a%d" % u) for u in range(2)]
+        for r in range(PACK):
+            nc.tensor.matmul_mx(
+                a_ps[r // 2][:, r % 2, :],
+                lhsT=q1c[:, r * P : (r + 1) * P].bitcast(FP8X4),
+                lhsT_scale=q1s[:, r * P : (r + 1) * P],
+                rhs=kw[:].bitcast(FP4X4),
+                rhs_scale=kb[:],
+                start=True,
+                stop=True,
+            )
+        pa = sb.tile([P, PAGE, PACK * G], F32, name="pa", tag="wide2")
+        z = sb.tile([P, PACK], F32, name="z")
+        for u in range(2):
+            neg_top = sb.tile([P, 2], F32, name="neg_top%d" % u)
+            nc.vector.tensor_reduce(neg_top[:], a_ps[u][:], axis=AX.X, op=ALU.max, negate=True)
+            for v in range(2):
+                r = 2 * u + v
+                nc.scalar.activation(
+                    pa[:, :, r * G : (r + 1) * G],
+                    a_ps[u][:, v, :].rearrange("p (g k) -> p k g", k=PAGE),
+                    ACT.Exp,
+                    bias=neg_top[:, v : v + 1],
+                    accum_out=z[:, r : r + 1],
+                )
+        sa_t_ps = page_sums(pa, "sa", "a0")
+        sa_t = sb.tile([P, P], F32, name="sa_t")
+        nc.scalar.copy(sa_t[:], sa_t_ps[:])
+        sa_ps = ps.tile([P, PACK, G], F32, name="sa_ps", tag="a0")
+        nc.tensor.transpose(sa_ps[:].rearrange("p r g -> p (r g)"), sa_t[:], ident[:])
+
+        pb = sb.tile([P, PAGE, G * PACK], F32, name="pb", tag="wide3")
+        for h in range(HALVES):
+            top = sb.tile([P, HG, PACK], F32, name="top%d" % h)
+            nc.vector.tensor_reduce(
+                top[:], b_ps[h][:].rearrange("p r (g k) -> p g r k", k=PAGE), axis=AX.X, op=ALU.max
+            )
+            shifted = sb.tile([P, PAGE, HG, PACK], F32, name="shifted%d" % h, tag="sh%d" % h, align_bytes=64)
+            nc.vector.tensor_tensor(
+                shifted[:],
+                b_ps[h][:].rearrange("p r (g k) -> p k g r", k=PAGE),
+                top[:].unsqueeze(1).to_broadcast([P, PAGE, HG, PACK]),
+                ALU.subtract,
+            )
+            nc.scalar.activation(
+                pb[:, :, h * HG * PACK : (h + 1) * HG * PACK], shifted[:].rearrange("p k g r -> p k (g r)"), ACT.Exp
+            )
+        sb_t_ps = page_sums(pb, "sb", "a1")
+        inv_t = sb.tile([P, P], F32, name="inv_t")
+        nc.vector.reciprocal(inv_t[:], sb_t_ps[:])
+        inv_ps = ps.tile([P, G, PACK], F32, name="inv_ps", tag="sb_turned_ps")
+        nc.tensor.transpose(inv_ps[:].rearrange("p g r -> p (g r)"), inv_t[:], ident[:])
+
+        z_inv = sb.tile([P, PACK], F32, name="z_inv")
+        nc.vector.reciprocal(z_inv[:], z[:])
+        row_factor = sb.tile([P, PACK], F32, name="row_factor")
+        nc.vector.tensor_tensor(row_factor[:], z_inv[:], row_scale[:], ALU.mult)
+        inv_row = sb.tile([P, G, PACK], F32, name="inv_row")
+        nc.vector.tensor_tensor(
+            inv_row[:], inv_ps[:], row_factor[:].unsqueeze(1).to_broadcast([P, G, PACK]), ALU.mult
+        )
+        factor = sb.tile([P, G, PACK], F32, name="factor")
+        nc.vector.tensor_tensor(factor[:], sa_ps[:].rearrange("p r g -> p g r"), inv_row[:], ALU.mult)
+
+        fade_ps = [ps.tile([P, PACK, P], F32, name="fade_ps%d" % h) for h in range(2)]
+        fade_sb = sb.tile([P, T], F32, name="fade_sb")
+        for h in range(2):
+            for c in range(PACK):
+                nc.tensor.transpose(fade_ps[h][:, c, :], fade_cols[:, h, c : c + 1].to_broadcast([P, P]), ident[:])
+            nc.scalar.copy(
+                fade_sb[:, h * BANK : (h + 1) * BANK].rearrange("p (n c) -> p n c", c=PACK),
+                fade_ps[h][:].rearrange("p c n -> p n c"),
+            )
+
+        g_parts = []
+        for h in range(2):
+            g_grouped = sb.tile([P, E // 2, PACK], BF16, name="g_grouped%d" % h, align_bytes=64, tag="sh%d" % h)
+            for v in range(2):
+                nc.scalar.copy(
+                    g_grouped[:, v * P : (v + 1) * P, :].rearrange("p (c i) j -> p c j i", i=4),
+                    g_raw[:, :, (2 * h + v) * P : (2 * h + v + 1) * P].rearrange("p j (c i) -> p c j i", i=4),
+                )
+            g_parts.append(quantise(g_grouped[:].rearrange("p e j -> p (e j)"), E // 2, "g%d" % h))
+
+        wq = sb.tile([P, PAGE, G * PACK], BF16, name="wq", align_bytes=64)
+        nc.vector.tensor_tensor(
+            wq[:],
+            pb[:],
+            factor[:].rearrange("p g r -> p (g r)").unsqueeze(1).to_broadcast([P, PAGE, G * PACK]),
+            ALU.mult,
+        )
+        wc, ws = quantise(wq[:].rearrange("p k c -> p (k c)"), I, "w")
+        gv_tags = ["bg0", "bg1", "a1", "a0"]
+        for j in range(4):
+            gc, gs = g_parts[j // 2]
+            gv_ps = ps.tile([P, PAGE, G], F32, name="gv_ps%d" % j, tag=gv_tags[j])
+            nc.tensor.matmul_mx(
+                gv_ps[:].rearrange("p k g -> p (k g)"),
+                lhsT=gc[:, j % 2 * P : (j % 2 + 1) * P].bitcast(FP8X4),
+                lhsT_scale=gs[:, j % 2 * P : (j % 2 + 1) * P],
+                rhs=wc[:].bitcast(FP8X4),
+                rhs_scale=ws[:],
+                start=True,
+                stop=True,
+            )
+            gv = sb.tile([P, G, PAGE], F32, name="gv%d" % j)
+            if j in VECTOR_COPIES:
+                nc.vector.tensor_copy(gv[:], gv_ps[:].rearrange("p k g -> p g k"))
+            else:
+                nc.scalar.copy(gv[:], gv_ps[:].rearrange("p k g -> p g k"))
+            src = gv[:].rearrange("p g k -> p (g k)")
+            if j in VECTOR_SCATTERS:
+                nc.vector.tensor_copy(gf[j][:].indirect(offsets[:]), src)
+            else:
+                nc.scalar.activation(gf[j][:].indirect(offsets[:]), src, ACT.Copy)
+
+        for j in range(GP_TILES):
+            for c0 in range(0, T, GP_COLS):
+                cols = slice(c0, c0 + GP_COLS)
+                nc.gpsimd.tensor_tensor(old_t[j][:, cols], old_t[j][:, cols], fade_sb[:, cols], ALU.mult)
+
+        faded = old_t[:GP_TILES]
+        for j in range(GP_TILES, 4):
+            faded.append(sb.tile([P, T], F32, name="faded%d" % j, tag="wide%d" % j))
+            for c0 in range(0, T, V_COLS):
+                h, n0 = divmod(c0, BANK)
+                piece = old_t[j][:, c0 : c0 + V_COLS].rearrange("p (n c) -> p n c", c=PACK)
+                fades = fade_ps[h][:, :, n0 // PACK : (n0 + V_COLS) // PACK].rearrange("p c n -> p n c")
+                dst = faded[j][:, c0 : c0 + V_COLS].rearrange("p (n c) -> p n c", c=PACK)
+                nc.vector.tensor_tensor(dst, piece, fades, ALU.mult)
+        for j in range(4):
+            for h in range(2):
+                cols = slice(h * BANK, (h + 1) * BANK)
+                nc.vector.tensor_tensor(faded[j][:, cols], faded[j][:, cols], gf[j][:, cols], ALU.add)
+                nc.sync.dma_start(out[j * P : (j + 1) * P, cols], faded[j][:, cols])

@@ -27,11 +27,11 @@ HG = G // HALVES
 BANK = 512
 GP_TILES = 2
 GP_COLS = 256
-Q2_VECTOR = 80
-Q1_VECTOR = 40
+Q2_VECTOR = (40, 40)
+Q1_VECTOR = (0, 32)
 V_COLS = 256
-VECTOR_COPIES = (0, 3)
-VECTOR_SCATTERS = (0,)
+VECTOR_COPIES = (1, 2)
+VECTOR_SCATTERS = (1,)
 
 
 def tile_attend_bpagethensecond_v_kernel(
@@ -46,33 +46,38 @@ def tile_attend_bpagethensecond_v_kernel(
         key_words = sb.tile([P, T], U16, name="key_words")
         key_bytes = sb.tile([P, T], U8, name="key_bytes")
         nc.gpsimd.memset(key_bytes[:].bitcast(I32), 0)
+        ident = sb.tile([P, P], F32, name="ident")
+        make_identity(nc, ident[:])
+        fade_cols = sb.tile([P, 2, PACK], F32, name="fade_cols")
+        nc.gpsimd.dma_start(fade_cols[:], fade.rearrange("o (h p c) -> p (o h) c", h=2, c=PACK))
+
+        def load_half(src, h, name):
+            raw = sb.tile([P, PACK, Q // 2], F32, name="%s_raw%d" % (name, h), tag="%s_raw%d" % (name, h))
+            cols = slice(h * (Q // 2), (h + 1) * (Q // 2))
+            nc.sync.dma_start(raw[:], src.rearrange("(p j) q -> p j q", j=PACK)[:, :, cols])
+            return raw
 
         nc.sync.dma_start(offsets[:], offs)
-        fade_cols = sb.tile([P, 2, PACK], F32, name="fade_cols")
-        nc.sync.dma_start(fade_cols[:], fade.rearrange("o (h p c) -> p (o h) c", h=2, c=PACK))
+        q2_raw = [load_half(query2, 0, "q2")]
         nc.sync.dma_start(key_words[:].bitcast(I32), keys_words[0].bitcast(I32))
         for u in range(4):
             nc.sync.dma_start(
                 key_bytes[32 * u : 32 * u + 4, :].bitcast(I32), keys_scales[0, 4 * u : 4 * u + 4, :].bitcast(I32)
             )
-        q2_raw = sb.tile([P, PACK, Q], F32, name="q2_raw")
-        nc.sync.dma_start(q2_raw[:], query2.rearrange("(p j) q -> p j q", j=PACK))
-        q1_raw = sb.tile([P, PACK, Q], F32, name="q1_raw")
-        nc.sync.dma_start(q1_raw[:], query.rearrange("(p j) q -> p j q", j=PACK))
+        q2_raw.append(load_half(query2, 1, "q2"))
+        q1_raw = [load_half(query, h, "q1") for h in range(2)]
         row_scale = sb.tile([P, PACK], F32, name="row_scale")
         nc.sync.dma_start(row_scale[:], qs.rearrange("(p j) o -> p (j o)", j=PACK))
         old_t = [sb.tile([P, T], F32, name="old%d" % j) for j in range(4)]
         g_raw = sb.tile([P, PACK, E], F32, name="g_raw")
         for j in range(4):
-            if j == 1:
+            if j == 2:
                 nc.sync.dma_start(g_raw[:], grows.rearrange("(p j) e -> p j e", j=PACK))
             nc.sync.dma_start(old_t[j][:], old[j * P : (j + 1) * P, :])
 
-        ident = sb.tile([P, P], F32, name="ident")
-        make_identity(nc, ident[:])
         gf = [sb.tile([P, T], F32, name="gf%d" % j) for j in range(4)]
         for j in range(4):
-            (nc.vector if j < 4 else nc.gpsimd).memset(gf[j][:], 0.0)
+            (nc.vector if j < 3 else nc.gpsimd).memset(gf[j][:], 0.0)
 
         kw = sb.tile([P, I], U16, name="kw", align_bytes=64)
         kb = sb.tile([P, I], U8, name="kb", align_bytes=64)
@@ -85,12 +90,14 @@ def tile_attend_bpagethensecond_v_kernel(
             nc.vector.quantize_mx(out=codes[:].bitcast(FP8X4), scales=scales[:], in_=grouped)
             return codes, scales
 
-        def deal(raw, name, split):
+        def deal(raw, name, splits):
             grouped = sb.tile([P, PACK, P, PACK], BF16, name=name, align_bytes=64)
-            dst = grouped[:].rearrange("p r m j -> p m j r")
-            src = raw[:].rearrange("p j (m r) -> p m j r", r=PACK)
-            nc.vector.tensor_copy(dst[:, :split], src[:, :split])
-            nc.scalar.copy(dst[:, split:], src[:, split:])
+            for h in range(2):
+                dst = grouped[:, :, h * 64 : (h + 1) * 64, :].rearrange("p r m j -> p m j r")
+                src = raw[h][:].rearrange("p j (m r) -> p m j r", r=PACK)
+                if splits[h] > 0:
+                    nc.vector.tensor_copy(dst[:, : splits[h]], src[:, : splits[h]])
+                nc.scalar.copy(dst[:, splits[h] :], src[:, splits[h] :])
             return quantise(grouped[:].rearrange("p r m j -> p (r m j)"), Q, name)
 
         def page_sums(tile, name, back_tag):
@@ -132,7 +139,32 @@ def tile_attend_bpagethensecond_v_kernel(
                 start=True,
                 stop=True,
             )
-        pa = sb.tile([P, PAGE, PACK * G], F32, name="pa", tag="wide2")
+        pb = sb.tile([P, PAGE, G * PACK], F32, name="pb", tag="pb", align_bytes=64)
+        top = [sb.tile([P, HG, PACK], F32, name="top%d" % h) for h in range(HALVES)]
+        for h in range(HALVES):
+            nc.vector.tensor_reduce(
+                top[h][:], b_ps[h][:].rearrange("p r (g k) -> p g r k", k=PAGE), axis=AX.X, op=ALU.max
+            )
+        for u in range(2):
+            places = slice(u * PAGE // 2, (u + 1) * PAGE // 2)
+            shifted = sb.tile([P, PAGE // 2, G, PACK], F32, name="shifted%d" % u, tag="sh%d" % u, align_bytes=64)
+            for h in range(HALVES):
+                nc.vector.tensor_tensor(
+                    shifted[:, :, h * HG : (h + 1) * HG, :],
+                    b_ps[h][:].rearrange("p r (g k) -> p k g r", k=PAGE)[:, places],
+                    top[h][:].unsqueeze(1).to_broadcast([P, PAGE // 2, HG, PACK]),
+                    ALU.subtract,
+                )
+            nc.scalar.activation(
+                pb[:, places, :].rearrange("p k c -> p (k c)"), shifted[:].rearrange("p k g r -> p (k g r)"), ACT.Exp
+            )
+        sb_t_ps = page_sums(pb, "sb", "a1")
+        inv_t = sb.tile([P, P], F32, name="inv_t")
+        nc.vector.reciprocal(inv_t[:], sb_t_ps[:])
+        inv_ps = ps.tile([P, G, PACK], F32, name="inv_ps", tag="sb_turned_ps")
+        nc.tensor.transpose(inv_ps[:].rearrange("p g r -> p (g r)"), inv_t[:], ident[:])
+
+        pa = sb.tile([P, PAGE, PACK * G], F32, name="pa")
         z = sb.tile([P, PACK], F32, name="z")
         for u in range(2):
             neg_top = sb.tile([P, 2], F32, name="neg_top%d" % u)
@@ -148,32 +180,9 @@ def tile_attend_bpagethensecond_v_kernel(
                 )
         sa_t_ps = page_sums(pa, "sa", "a0")
         sa_t = sb.tile([P, P], F32, name="sa_t")
-        nc.scalar.copy(sa_t[:], sa_t_ps[:])
+        nc.vector.tensor_copy(sa_t[:], sa_t_ps[:])
         sa_ps = ps.tile([P, PACK, G], F32, name="sa_ps", tag="a0")
         nc.tensor.transpose(sa_ps[:].rearrange("p r g -> p (r g)"), sa_t[:], ident[:])
-
-        pb = sb.tile([P, PAGE, G * PACK], F32, name="pb", tag="wide3")
-        for h in range(HALVES):
-            top = sb.tile([P, HG, PACK], F32, name="top%d" % h)
-            nc.vector.tensor_reduce(
-                top[:], b_ps[h][:].rearrange("p r (g k) -> p g r k", k=PAGE), axis=AX.X, op=ALU.max
-            )
-            shifted = sb.tile([P, PAGE, HG, PACK], F32, name="shifted%d" % h, tag="sh%d" % h, align_bytes=64)
-            nc.vector.tensor_tensor(
-                shifted[:],
-                b_ps[h][:].rearrange("p r (g k) -> p k g r", k=PAGE),
-                top[:].unsqueeze(1).to_broadcast([P, PAGE, HG, PACK]),
-                ALU.subtract,
-            )
-            nc.scalar.activation(
-                pb[:, :, h * HG * PACK : (h + 1) * HG * PACK], shifted[:].rearrange("p k g r -> p k (g r)"), ACT.Exp
-            )
-        sb_t_ps = page_sums(pb, "sb", "a1")
-        inv_t = sb.tile([P, P], F32, name="inv_t")
-        nc.vector.reciprocal(inv_t[:], sb_t_ps[:])
-        inv_ps = ps.tile([P, G, PACK], F32, name="inv_ps", tag="sb_turned_ps")
-        nc.tensor.transpose(inv_ps[:].rearrange("p g r -> p (g r)"), inv_t[:], ident[:])
-
         z_inv = sb.tile([P, PACK], F32, name="z_inv")
         nc.vector.reciprocal(z_inv[:], z[:])
         row_factor = sb.tile([P, PACK], F32, name="row_factor")
@@ -186,26 +195,26 @@ def tile_attend_bpagethensecond_v_kernel(
         nc.vector.tensor_tensor(factor[:], sa_ps[:].rearrange("p r g -> p g r"), inv_row[:], ALU.mult)
 
         fade_ps = [ps.tile([P, PACK, P], F32, name="fade_ps%d" % h) for h in range(2)]
-        fade_sb = sb.tile([P, T], F32, name="fade_sb")
+        fade_sb = sb.tile([P, 2, BANK], F32, name="fade_sb", tag="q1_raw1")
         for h in range(2):
             for c in range(PACK):
                 nc.tensor.transpose(fade_ps[h][:, c, :], fade_cols[:, h, c : c + 1].to_broadcast([P, P]), ident[:])
             nc.scalar.copy(
-                fade_sb[:, h * BANK : (h + 1) * BANK].rearrange("p (n c) -> p n c", c=PACK),
+                fade_sb[:, h, :].rearrange("p (n c) -> p n c", c=PACK),
                 fade_ps[h][:].rearrange("p c n -> p n c"),
             )
 
-        g_parts = []
-        for h in range(2):
-            g_grouped = sb.tile([P, E // 2, PACK], BF16, name="g_grouped%d" % h, align_bytes=64, tag="sh%d" % h)
-            for v in range(2):
-                nc.scalar.copy(
-                    g_grouped[:, v * P : (v + 1) * P, :].rearrange("p (c i) j -> p c j i", i=4),
-                    g_raw[:, :, (2 * h + v) * P : (2 * h + v + 1) * P].rearrange("p j (c i) -> p c j i", i=4),
-                )
-            g_parts.append(quantise(g_grouped[:].rearrange("p e j -> p (e j)"), E // 2, "g%d" % h))
+        g_grouped = [
+            sb.tile([P, E // 2, PACK], BF16, name="g_grouped%d" % h, align_bytes=64, tag="sh%d" % (1 - h)) for h in range(2)
+        ]
+        for v in range(4):
+            nc.scalar.copy(
+                g_grouped[v // 2][:, v % 2 * P : (v % 2 + 1) * P, :].rearrange("p (c i) j -> p c j i", i=4),
+                g_raw[:, :, v * P : (v + 1) * P].rearrange("p j (c i) -> p c j i", i=4),
+            )
+        g_parts = [quantise(g_grouped[0][:].rearrange("p e j -> p (e j)"), E // 2, "g0")]
 
-        wq = sb.tile([P, PAGE, G * PACK], BF16, name="wq", align_bytes=64)
+        wq = sb.tile([P, PAGE, G * PACK], BF16, name="wq", tag="late", align_bytes=64)
         nc.vector.tensor_tensor(
             wq[:],
             pb[:],
@@ -213,12 +222,13 @@ def tile_attend_bpagethensecond_v_kernel(
             ALU.mult,
         )
         wc, ws = quantise(wq[:].rearrange("p k c -> p (k c)"), I, "w")
+        g_parts.append(quantise(g_grouped[1][:].rearrange("p e j -> p (e j)"), E // 2, "g1"))
         gv_tags = ["bg0", "bg1", "a1", "a0"]
+        gv_ps = [ps.tile([P, PAGE, G], F32, name="gv_ps%d" % j, tag=gv_tags[j]) for j in range(4)]
         for j in range(4):
             gc, gs = g_parts[j // 2]
-            gv_ps = ps.tile([P, PAGE, G], F32, name="gv_ps%d" % j, tag=gv_tags[j])
             nc.tensor.matmul_mx(
-                gv_ps[:].rearrange("p k g -> p (k g)"),
+                gv_ps[j][:].rearrange("p k g -> p (k g)"),
                 lhsT=gc[:, j % 2 * P : (j % 2 + 1) * P].bitcast(FP8X4),
                 lhsT_scale=gs[:, j % 2 * P : (j % 2 + 1) * P],
                 rhs=wc[:].bitcast(FP8X4),
@@ -226,33 +236,36 @@ def tile_attend_bpagethensecond_v_kernel(
                 start=True,
                 stop=True,
             )
-            gv = sb.tile([P, G, PAGE], F32, name="gv%d" % j)
-            if j in VECTOR_COPIES:
-                nc.vector.tensor_copy(gv[:], gv_ps[:].rearrange("p k g -> p g k"))
-            else:
-                nc.scalar.copy(gv[:], gv_ps[:].rearrange("p k g -> p g k"))
-            src = gv[:].rearrange("p g k -> p (g k)")
-            if j in VECTOR_SCATTERS:
-                nc.vector.tensor_copy(gf[j][:].indirect(offsets[:]), src)
-            else:
-                nc.scalar.activation(gf[j][:].indirect(offsets[:]), src, ACT.Copy)
 
-        for j in range(GP_TILES):
+        def leave_psum(j, copy, tag):
+            gv = sb.tile([P, G, PAGE], F32, name="gv%d" % j, tag=tag)
+            copy(gv[:], gv_ps[j][:].rearrange("p k g -> p g k"))
+            return gv[:].rearrange("p g k -> p (g k)")
+
+        gv0 = leave_psum(0, nc.scalar.copy, "gv_scalar")
+        nc.scalar.activation(gf[0][:].indirect(offsets[:]), gv0, ACT.Copy)
+        gv1 = leave_psum(1, nc.vector.tensor_copy, "gv1")
+        gv2 = leave_psum(2, nc.vector.tensor_copy, "gv2")
+        nc.vector.tensor_copy(gf[1][:].indirect(offsets[:]), gv1)
+        gv3 = leave_psum(3, nc.scalar.copy, "gv_scalar")
+        nc.scalar.activation(gf[2][:].indirect(offsets[:]), gv2, ACT.Copy)
+        nc.scalar.activation(gf[3][:].indirect(offsets[:]), gv3, ACT.Copy)
+
+        faded = old_t[:3] + [sb.tile([P, T], F32, name="faded3", tag="late", align_bytes=64)]
+        for j in range(4):
             for c0 in range(0, T, GP_COLS):
                 cols = slice(c0, c0 + GP_COLS)
-                nc.gpsimd.tensor_tensor(old_t[j][:, cols], old_t[j][:, cols], fade_sb[:, cols], ALU.mult)
-
-        faded = old_t[:GP_TILES]
-        for j in range(GP_TILES, 4):
-            faded.append(sb.tile([P, T], F32, name="faded%d" % j, tag="wide%d" % j))
-            for c0 in range(0, T, V_COLS):
                 h, n0 = divmod(c0, BANK)
-                piece = old_t[j][:, c0 : c0 + V_COLS].rearrange("p (n c) -> p n c", c=PACK)
-                fades = fade_ps[h][:, :, n0 // PACK : (n0 + V_COLS) // PACK].rearrange("p c n -> p n c")
-                dst = faded[j][:, c0 : c0 + V_COLS].rearrange("p (n c) -> p n c", c=PACK)
-                nc.vector.tensor_tensor(dst, piece, fades, ALU.mult)
+                if j >= 2 and c0 >= (0, 512)[j - 2]:
+                    piece = old_t[j][:, cols].rearrange("p (n c) -> p n c", c=PACK)
+                    fades = fade_ps[h][:, :, n0 // PACK : (n0 + GP_COLS) // PACK].rearrange("p c n -> p n c")
+                    nc.vector.tensor_tensor(faded[j][:, cols].rearrange("p (n c) -> p n c", c=PACK), piece, fades, ALU.mult)
+                else:
+                    nc.gpsimd.tensor_tensor(faded[j][:, cols], old_t[j][:, cols], fade_sb[:, h, n0 : n0 + GP_COLS], ALU.mult)
+
         for j in range(4):
-            for h in range(2):
-                cols = slice(h * BANK, (h + 1) * BANK)
+            edges = [0, BANK, T] if j < 3 else [0, BANK, 3 * T // 4, T]
+            for c0, c1 in zip(edges, edges[1:]):
+                cols = slice(c0, c1)
                 nc.vector.tensor_tensor(faded[j][:, cols], faded[j][:, cols], gf[j][:, cols], ALU.add)
                 nc.sync.dma_start(out[j * P : (j + 1) * P, cols], faded[j][:, cols])

@@ -27,8 +27,8 @@ HG = G // HALVES
 BANK = 512
 GP_TILES = 2
 GP_COLS = 256
-Q2_VECTOR = (40, 40)
-Q1_VECTOR = (0, 32)
+Q2_VECTOR = 88
+Q1_VECTOR = 48
 V_COLS = 256
 VECTOR_COPIES = (1, 2)
 VECTOR_SCATTERS = (1,)
@@ -48,36 +48,31 @@ def tile_attend_bpagethensecond_v_kernel(
         nc.gpsimd.memset(key_bytes[:].bitcast(I32), 0)
         ident = sb.tile([P, P], F32, name="ident")
         make_identity(nc, ident[:])
-        fade_cols = sb.tile([P, 2, PACK], F32, name="fade_cols")
-        nc.gpsimd.dma_start(fade_cols[:], fade.rearrange("o (h p c) -> p (o h) c", h=2, c=PACK))
-
-        def load_half(src, h, name):
-            raw = sb.tile([P, PACK, Q // 2], F32, name="%s_raw%d" % (name, h), tag="%s_raw%d" % (name, h))
-            cols = slice(h * (Q // 2), (h + 1) * (Q // 2))
-            nc.sync.dma_start(raw[:], src.rearrange("(p j) q -> p j q", j=PACK)[:, :, cols])
-            return raw
 
         nc.sync.dma_start(offsets[:], offs)
-        q2_raw = [load_half(query2, 0, "q2")]
+        fade_cols = sb.tile([P, 2, PACK], F32, name="fade_cols")
+        nc.sync.dma_start(fade_cols[:], fade.rearrange("o (h p c) -> p (o h) c", h=2, c=PACK))
         nc.sync.dma_start(key_words[:].bitcast(I32), keys_words[0].bitcast(I32))
         for u in range(4):
             nc.sync.dma_start(
                 key_bytes[32 * u : 32 * u + 4, :].bitcast(I32), keys_scales[0, 4 * u : 4 * u + 4, :].bitcast(I32)
             )
-        q2_raw.append(load_half(query2, 1, "q2"))
-        q1_raw = [load_half(query, h, "q1") for h in range(2)]
+        q2_raw = sb.tile([P, PACK, Q], F32, name="q2_raw")
+        nc.sync.dma_start(q2_raw[:], query2.rearrange("(p j) q -> p j q", j=PACK))
+        q1_raw = sb.tile([P, PACK, Q], F32, name="q1_raw")
+        nc.sync.dma_start(q1_raw[:], query.rearrange("(p j) q -> p j q", j=PACK))
         row_scale = sb.tile([P, PACK], F32, name="row_scale")
         nc.sync.dma_start(row_scale[:], qs.rearrange("(p j) o -> p (j o)", j=PACK))
         old_t = [sb.tile([P, T], F32, name="old%d" % j) for j in range(4)]
         g_raw = sb.tile([P, PACK, E], F32, name="g_raw")
         for j in range(4):
-            if j == 2:
+            if j == 1:
                 nc.sync.dma_start(g_raw[:], grows.rearrange("(p j) e -> p j e", j=PACK))
             nc.sync.dma_start(old_t[j][:], old[j * P : (j + 1) * P, :])
 
         gf = [sb.tile([P, T], F32, name="gf%d" % j) for j in range(4)]
         for j in range(4):
-            (nc.vector if j < 3 else nc.gpsimd).memset(gf[j][:], 0.0)
+            (nc.vector if j < 4 else nc.gpsimd).memset(gf[j][:], 0.0)
 
         kw = sb.tile([P, I], U16, name="kw", align_bytes=64)
         kb = sb.tile([P, I], U8, name="kb", align_bytes=64)
@@ -90,14 +85,12 @@ def tile_attend_bpagethensecond_v_kernel(
             nc.vector.quantize_mx(out=codes[:].bitcast(FP8X4), scales=scales[:], in_=grouped)
             return codes, scales
 
-        def deal(raw, name, splits):
-            grouped = sb.tile([P, PACK, P, PACK], BF16, name=name, align_bytes=64)
-            for h in range(2):
-                dst = grouped[:, :, h * 64 : (h + 1) * 64, :].rearrange("p r m j -> p m j r")
-                src = raw[h][:].rearrange("p j (m r) -> p m j r", r=PACK)
-                if splits[h] > 0:
-                    nc.vector.tensor_copy(dst[:, : splits[h]], src[:, : splits[h]])
-                nc.scalar.copy(dst[:, splits[h] :], src[:, splits[h] :])
+        def deal(raw, name, split):
+            grouped = sb.tile([P, PACK, P, PACK], BF16, name=name, tag=name, align_bytes=64)
+            dst = grouped[:].rearrange("p r m j -> p m j r")
+            src = raw[:].rearrange("p j (m r) -> p m j r", r=PACK)
+            nc.vector.tensor_copy(dst[:, :split], src[:, :split])
+            nc.scalar.copy(dst[:, split:], src[:, split:])
             return quantise(grouped[:].rearrange("p r m j -> p (r m j)"), Q, name)
 
         def page_sums(tile, name, back_tag):
@@ -195,7 +188,7 @@ def tile_attend_bpagethensecond_v_kernel(
         nc.vector.tensor_tensor(factor[:], sa_ps[:].rearrange("p r g -> p g r"), inv_row[:], ALU.mult)
 
         fade_ps = [ps.tile([P, PACK, P], F32, name="fade_ps%d" % h) for h in range(2)]
-        fade_sb = sb.tile([P, 2, BANK], F32, name="fade_sb", tag="q1_raw1")
+        fade_sb = sb.tile([P, 2, BANK], F32, name="fade_sb")
         for h in range(2):
             for c in range(PACK):
                 nc.tensor.transpose(fade_ps[h][:, c, :], fade_cols[:, h, c : c + 1].to_broadcast([P, P]), ident[:])
@@ -223,12 +216,12 @@ def tile_attend_bpagethensecond_v_kernel(
         )
         wc, ws = quantise(wq[:].rearrange("p k c -> p (k c)"), I, "w")
         g_parts.append(quantise(g_grouped[1][:].rearrange("p e j -> p (e j)"), E // 2, "g1"))
-        gv_tags = ["bg0", "bg1", "a1", "a0"]
-        gv_ps = [ps.tile([P, PAGE, G], F32, name="gv_ps%d" % j, tag=gv_tags[j]) for j in range(4)]
-        for j in range(4):
+
+        def leave_psum(j, copy, bank):
             gc, gs = g_parts[j // 2]
+            gv_ps = ps.tile([P, PAGE, G], F32, name="gv_ps%d" % j, tag=bank)
             nc.tensor.matmul_mx(
-                gv_ps[j][:].rearrange("p k g -> p (k g)"),
+                gv_ps[:].rearrange("p k g -> p (k g)"),
                 lhsT=gc[:, j % 2 * P : (j % 2 + 1) * P].bitcast(FP8X4),
                 lhsT_scale=gs[:, j % 2 * P : (j % 2 + 1) * P],
                 rhs=wc[:].bitcast(FP8X4),
@@ -236,27 +229,26 @@ def tile_attend_bpagethensecond_v_kernel(
                 start=True,
                 stop=True,
             )
-
-        def leave_psum(j, copy, tag):
-            gv = sb.tile([P, G, PAGE], F32, name="gv%d" % j, tag=tag)
-            copy(gv[:], gv_ps[j][:].rearrange("p k g -> p g k"))
+            gv = sb.tile([P, G, PAGE], F32, name="gv%d" % j)
+            copy(gv[:], gv_ps[:].rearrange("p k g -> p g k"))
             return gv[:].rearrange("p g k -> p (g k)")
 
-        gv0 = leave_psum(0, nc.scalar.copy, "gv_scalar")
+        gv0 = leave_psum(0, nc.scalar.copy, "bg0")
         nc.scalar.activation(gf[0][:].indirect(offsets[:]), gv0, ACT.Copy)
-        gv1 = leave_psum(1, nc.vector.tensor_copy, "gv1")
-        gv2 = leave_psum(2, nc.vector.tensor_copy, "gv2")
+        gv1 = leave_psum(1, nc.vector.tensor_copy, "bg1")
+        gv2 = leave_psum(2, nc.vector.tensor_copy, "a1")
         nc.vector.tensor_copy(gf[1][:].indirect(offsets[:]), gv1)
-        gv3 = leave_psum(3, nc.scalar.copy, "gv_scalar")
+        gv3 = leave_psum(3, nc.scalar.copy, "bg0")
         nc.scalar.activation(gf[2][:].indirect(offsets[:]), gv2, ACT.Copy)
         nc.scalar.activation(gf[3][:].indirect(offsets[:]), gv3, ACT.Copy)
 
-        faded = old_t[:3] + [sb.tile([P, T], F32, name="faded3", tag="late", align_bytes=64)]
+        faded = [sb.tile([P, T], F32, name="faded0", tag="q1", align_bytes=64)] + old_t[1:3]
+        faded.append(sb.tile([P, T], F32, name="faded3"))
         for j in range(4):
             for c0 in range(0, T, GP_COLS):
                 cols = slice(c0, c0 + GP_COLS)
                 h, n0 = divmod(c0, BANK)
-                if j >= 2 and c0 >= (0, 512)[j - 2]:
+                if c0 >= (1024, 768, 0, 0)[j]:
                     piece = old_t[j][:, cols].rearrange("p (n c) -> p n c", c=PACK)
                     fades = fade_ps[h][:, :, n0 // PACK : (n0 + GP_COLS) // PACK].rearrange("p c n -> p n c")
                     nc.vector.tensor_tensor(faded[j][:, cols].rearrange("p (n c) -> p n c", c=PACK), piece, fades, ALU.mult)

@@ -21,17 +21,14 @@ AX = mybir.AxisListType
 P = 128
 PACK = 4
 PAGE = I // G
-HALVES = 2
-HS = I // HALVES
-HG = G // HALVES
+HS = I // 2
+HG = G // 2
 BANK = 512
-GP_TILES = 2
-GP_COLS = 256
+BLOCKS = T // P
+PIECE = 256
 Q2_VECTOR = 88
 Q1_VECTOR = 48
-V_COLS = 256
-VECTOR_COPIES = (1, 2)
-VECTOR_SCATTERS = (1,)
+TURNED = (2, 3)
 
 
 def tile_attend_bpagethensecond_v_kernel(
@@ -45,39 +42,39 @@ def tile_attend_bpagethensecond_v_kernel(
         offsets = sb.tile([P, I // 16], U16, name="offsets")
         key_words = sb.tile([P, T], U16, name="key_words")
         key_bytes = sb.tile([P, T], U8, name="key_bytes")
+        fade_rows = sb.tile([P, P], F32, name="fade_rows")
         nc.gpsimd.memset(key_bytes[:].bitcast(I32), 0)
+        nc.gpsimd.memset(fade_rows[:], 0.0)
         ident = sb.tile([P, P], F32, name="ident")
         make_identity(nc, ident[:])
 
         nc.sync.dma_start(offsets[:], offs)
-        fade_cols = sb.tile([P, 2, PACK], F32, name="fade_cols")
-        nc.sync.dma_start(fade_cols[:], fade.rearrange("o (h p c) -> p (o h) c", h=2, c=PACK))
         nc.sync.dma_start(key_words[:].bitcast(I32), keys_words[0].bitcast(I32))
         for u in range(4):
             nc.sync.dma_start(
                 key_bytes[32 * u : 32 * u + 4, :].bitcast(I32), keys_scales[0, 4 * u : 4 * u + 4, :].bitcast(I32)
             )
+        nc.sync.dma_start(fade_rows[0:BLOCKS, :], fade.rearrange("o (c n) -> (o c) n", n=P))
         q2_raw = sb.tile([P, PACK, Q], F32, name="q2_raw")
         nc.sync.dma_start(q2_raw[:], query2.rearrange("(p j) q -> p j q", j=PACK))
         q1_raw = sb.tile([P, PACK, Q], F32, name="q1_raw")
         nc.sync.dma_start(q1_raw[:], query.rearrange("(p j) q -> p j q", j=PACK))
         row_scale = sb.tile([P, PACK], F32, name="row_scale")
         nc.sync.dma_start(row_scale[:], qs.rearrange("(p j) o -> p (j o)", j=PACK))
-        old_t = [sb.tile([P, T], F32, name="old%d" % j) for j in range(4)]
         g_raw = sb.tile([P, PACK, E], F32, name="g_raw")
-        for j in range(4):
-            if j == 1:
+        old_t = [sb.tile([P, T], F32, name="old%d" % j) for j in range(4)]
+        for n, j in enumerate((2, 3, 0, 1)):
+            if n == 0:
                 nc.sync.dma_start(g_raw[:], grows.rearrange("(p j) e -> p j e", j=PACK))
             nc.sync.dma_start(old_t[j][:], old[j * P : (j + 1) * P, :])
 
         gf = [sb.tile([P, T], F32, name="gf%d" % j) for j in range(4)]
         for j in range(4):
-            (nc.vector if j < 4 else nc.gpsimd).memset(gf[j][:], 0.0)
+            nc.vector.memset(gf[j][:], 0.0)
 
         kw = sb.tile([P, I], U16, name="kw", align_bytes=64)
         kb = sb.tile([P, I], U8, name="kb", align_bytes=64)
         nc.vector.tensor_copy(kw[:], key_words[:].indirect(offsets[:]))
-        nc.vector.tensor_copy(kb[:], key_bytes[:].indirect(offsets[:]))
 
         def quantise(grouped, words, name):
             codes = sb.tile([P, words], U32, name=name + "_codes", align_bytes=64)
@@ -86,15 +83,15 @@ def tile_attend_bpagethensecond_v_kernel(
             return codes, scales
 
         def deal(raw, name, split):
-            grouped = sb.tile([P, PACK, P, PACK], BF16, name=name, tag=name, align_bytes=64)
+            grouped = sb.tile([P, PACK, P, PACK], BF16, name=name, align_bytes=64)
             dst = grouped[:].rearrange("p r m j -> p m j r")
             src = raw[:].rearrange("p j (m r) -> p m j r", r=PACK)
             nc.vector.tensor_copy(dst[:, :split], src[:, :split])
             nc.scalar.copy(dst[:, split:], src[:, split:])
-            return quantise(grouped[:].rearrange("p r m j -> p (r m j)"), Q, name)
+            return grouped[:].rearrange("p r m j -> p (r m j)")
 
-        def page_sums(tile, name, back_tag):
-            turned_ps = ps.tile([P, P], F32, name=name + "_turned_ps")
+        def page_sums(tile, name):
+            turned_ps = ps.tile([P, P], F32, name=name, tag=name)
             for k in range(PAGE):
                 nc.tensor.matmul(
                     turned_ps[:],
@@ -106,9 +103,11 @@ def tile_attend_bpagethensecond_v_kernel(
                 )
             return turned_ps
 
-        q2c, q2s = deal(q2_raw, "q2", Q2_VECTOR)
-        b_ps = [ps.tile([P, PACK, HS], F32, name="b_ps%d" % h, tag="bg%d" % h) for h in range(HALVES)]
-        for h in range(HALVES):
+        q2_dealt = deal(q2_raw, "q2", Q2_VECTOR)
+        nc.vector.tensor_copy(kb[:], key_bytes[:].indirect(offsets[:]))
+        q2c, q2s = quantise(q2_dealt, Q, "q2")
+        b_ps = [ps.tile([P, PACK, HS], F32, name="b_ps%d" % h, tag="b%d" % h) for h in range(2)]
+        for h in range(2):
             for r in range(PACK):
                 nc.tensor.matmul_mx(
                     b_ps[h][:, r, :],
@@ -120,7 +119,7 @@ def tile_attend_bpagethensecond_v_kernel(
                     stop=True,
                 )
 
-        q1c, q1s = deal(q1_raw, "q1", Q1_VECTOR)
+        q1c, q1s = quantise(deal(q1_raw, "q1", Q1_VECTOR), Q, "q1")
         a_ps = [ps.tile([P, 2, I], F32, name="a_ps%d" % u, tag="a%d" % u) for u in range(2)]
         for r in range(PACK):
             nc.tensor.matmul_mx(
@@ -132,16 +131,17 @@ def tile_attend_bpagethensecond_v_kernel(
                 start=True,
                 stop=True,
             )
-        pb = sb.tile([P, PAGE, G * PACK], F32, name="pb", tag="pb", align_bytes=64)
-        top = [sb.tile([P, HG, PACK], F32, name="top%d" % h) for h in range(HALVES)]
-        for h in range(HALVES):
+
+        pb = sb.tile([P, PAGE, G * PACK], F32, name="pb")
+        top = [sb.tile([P, HG, PACK], F32, name="top%d" % h) for h in range(2)]
+        for h in range(2):
             nc.vector.tensor_reduce(
                 top[h][:], b_ps[h][:].rearrange("p r (g k) -> p g r k", k=PAGE), axis=AX.X, op=ALU.max
             )
         for u in range(2):
             places = slice(u * PAGE // 2, (u + 1) * PAGE // 2)
             shifted = sb.tile([P, PAGE // 2, G, PACK], F32, name="shifted%d" % u, tag="sh%d" % u, align_bytes=64)
-            for h in range(HALVES):
+            for h in range(2):
                 nc.vector.tensor_tensor(
                     shifted[:, :, h * HG : (h + 1) * HG, :],
                     b_ps[h][:].rearrange("p r (g k) -> p k g r", k=PAGE)[:, places],
@@ -151,13 +151,14 @@ def tile_attend_bpagethensecond_v_kernel(
             nc.scalar.activation(
                 pb[:, places, :].rearrange("p k c -> p (k c)"), shifted[:].rearrange("p k g r -> p (k g r)"), ACT.Exp
             )
-        sb_t_ps = page_sums(pb, "sb", "a1")
+        sb_t_ps = page_sums(pb, "sum_b")
         inv_t = sb.tile([P, P], F32, name="inv_t")
         nc.vector.reciprocal(inv_t[:], sb_t_ps[:])
-        inv_ps = ps.tile([P, G, PACK], F32, name="inv_ps", tag="sb_turned_ps")
+        inv_ps = ps.tile([P, G, PACK], F32, name="inv_ps", tag="sum_b")
         nc.tensor.transpose(inv_ps[:].rearrange("p g r -> p (g r)"), inv_t[:], ident[:])
 
-        pa = sb.tile([P, PAGE, PACK * G], F32, name="pa")
+        pa = sb.tile([P, PACK, G, PAGE], F32, name="pa")
+        sa = sb.tile([P, PACK, G], F32, name="sa")
         z = sb.tile([P, PACK], F32, name="z")
         for u in range(2):
             neg_top = sb.tile([P, 2], F32, name="neg_top%d" % u)
@@ -165,40 +166,37 @@ def tile_attend_bpagethensecond_v_kernel(
             for v in range(2):
                 r = 2 * u + v
                 nc.scalar.activation(
-                    pa[:, :, r * G : (r + 1) * G],
-                    a_ps[u][:, v, :].rearrange("p (g k) -> p k g", k=PAGE),
+                    pa[:, r].rearrange("p g k -> p (g k)"),
+                    a_ps[u][:, v, :],
                     ACT.Exp,
                     bias=neg_top[:, v : v + 1],
                     accum_out=z[:, r : r + 1],
                 )
-        sa_t_ps = page_sums(pa, "sa", "a0")
-        sa_t = sb.tile([P, P], F32, name="sa_t")
-        nc.vector.tensor_copy(sa_t[:], sa_t_ps[:])
-        sa_ps = ps.tile([P, PACK, G], F32, name="sa_ps", tag="a0")
-        nc.tensor.transpose(sa_ps[:].rearrange("p r g -> p (r g)"), sa_t[:], ident[:])
         z_inv = sb.tile([P, PACK], F32, name="z_inv")
         nc.vector.reciprocal(z_inv[:], z[:])
         row_factor = sb.tile([P, PACK], F32, name="row_factor")
         nc.vector.tensor_tensor(row_factor[:], z_inv[:], row_scale[:], ALU.mult)
-        inv_row = sb.tile([P, G, PACK], F32, name="inv_row")
+        for r in range(0, PACK, 1):
+            nc.vector.tensor_reduce(sa[:, r : r + 1], pa[:, r : r + 1], axis=AX.X, op=ALU.add)
+        share = sb.tile([P, G, PACK], F32, name="share")
         nc.vector.tensor_tensor(
-            inv_row[:], inv_ps[:], row_factor[:].unsqueeze(1).to_broadcast([P, G, PACK]), ALU.mult
+            share[:], sa[:].rearrange("p r g -> p g r"), row_factor[:].unsqueeze(1).to_broadcast([P, G, PACK]), ALU.mult
         )
         factor = sb.tile([P, G, PACK], F32, name="factor")
-        nc.vector.tensor_tensor(factor[:], sa_ps[:].rearrange("p r g -> p g r"), inv_row[:], ALU.mult)
+        nc.vector.tensor_tensor(factor[:], inv_ps[:], share[:], ALU.mult)
 
-        fade_ps = [ps.tile([P, PACK, P], F32, name="fade_ps%d" % h) for h in range(2)]
-        fade_sb = sb.tile([P, 2, BANK], F32, name="fade_sb")
-        for h in range(2):
-            for c in range(PACK):
-                nc.tensor.transpose(fade_ps[h][:, c, :], fade_cols[:, h, c : c + 1].to_broadcast([P, P]), ident[:])
-            nc.scalar.copy(
-                fade_sb[:, h, :].rearrange("p (n c) -> p n c", c=PACK),
-                fade_ps[h][:].rearrange("p c n -> p n c"),
+        cols_ps = ps.tile([P, P], F32, name="cols_ps", tag="f1")
+        nc.tensor.transpose(cols_ps[:], fade_rows[:], ident[:])
+        fade_cols = sb.tile([P, BLOCKS], F32, name="fade_cols")
+        nc.scalar.copy(fade_cols[:], cols_ps[:, 0:BLOCKS])
+        fade_ps = [ps.tile([P, BANK], F32, name="fade_ps%d" % h, tag="f%d" % h) for h in range(2)]
+        for c in range(BLOCKS):
+            nc.tensor.transpose(
+                fade_ps[c // 4][:, c % 4 * P : (c % 4 + 1) * P], fade_cols[:, c : c + 1].to_broadcast([P, P]), ident[:]
             )
 
         g_grouped = [
-            sb.tile([P, E // 2, PACK], BF16, name="g_grouped%d" % h, align_bytes=64, tag="sh%d" % (1 - h)) for h in range(2)
+            sb.tile([P, E // 2, PACK], BF16, name="g_grouped%d" % h, align_bytes=64, tag=("g0", "sh1")[h]) for h in range(2)
         ]
         for v in range(4):
             nc.scalar.copy(
@@ -207,7 +205,7 @@ def tile_attend_bpagethensecond_v_kernel(
             )
         g_parts = [quantise(g_grouped[0][:].rearrange("p e j -> p (e j)"), E // 2, "g0")]
 
-        wq = sb.tile([P, PAGE, G * PACK], BF16, name="wq", tag="late", align_bytes=64)
+        wq = sb.tile([P, PAGE, G * PACK], BF16, name="wq", align_bytes=64)
         nc.vector.tensor_tensor(
             wq[:],
             pb[:],
@@ -217,47 +215,66 @@ def tile_attend_bpagethensecond_v_kernel(
         wc, ws = quantise(wq[:].rearrange("p k c -> p (k c)"), I, "w")
         g_parts.append(quantise(g_grouped[1][:].rearrange("p e j -> p (e j)"), E // 2, "g1"))
 
-        def leave_psum(j, copy, bank):
-            gc, gs = g_parts[j // 2]
-            gv_ps = ps.tile([P, PAGE, G], F32, name="gv_ps%d" % j, tag=bank)
-            nc.tensor.matmul_mx(
-                gv_ps[:].rearrange("p k g -> p (k g)"),
-                lhsT=gc[:, j % 2 * P : (j % 2 + 1) * P].bitcast(FP8X4),
-                lhsT_scale=gs[:, j % 2 * P : (j % 2 + 1) * P],
-                rhs=wc[:].bitcast(FP8X4),
-                rhs_scale=ws[:],
-                start=True,
-                stop=True,
-            )
-            gv = sb.tile([P, G, PAGE], F32, name="gv%d" % j)
-            copy(gv[:], gv_ps[:].rearrange("p k g -> p g k"))
-            return gv[:].rearrange("p g k -> p (g k)")
+        nt = len(TURNED)
+        scaled = []
+        for c0 in range(0, BLOCKS, 2):
+            stage = ps.tile([P, 2, nt, P], F32, name="stage%d" % c0, tag="b%d" % (c0 // 2 % 2))
+            for c in range(2):
+                for n, j in enumerate(TURNED):
+                    nc.tensor.transpose(stage[:, c, n, :], old_t[j][:, (c0 + c) * P : (c0 + c + 1) * P], ident[:])
+            for c in range(2):
+                block = sb.tile([P, nt, P], F32, name="scaled%d" % (c0 + c))
+                nc.scalar.activation(block[:], stage[:, c], ACT.Copy, scale=fade_cols[:, c0 + c : c0 + c + 1])
+                scaled.append(block)
+        faded = {}
 
-        gv0 = leave_psum(0, nc.scalar.copy, "bg0")
+        def turn_back(n, banks):
+            for h in range(2):
+                back = ps.tile([P, BANK], F32, name="back%d%d" % (n, h), tag=banks[h])
+                for c in range(4):
+                    nc.tensor.transpose(back[:, c * P : (c + 1) * P], scaled[4 * h + c][:, n, :], ident[:])
+                faded[TURNED[n], h] = back
+
+        turn_back(0, ("a0", "a1"))
+        for j in range(4):
+            if j not in TURNED:
+                for c0 in range(0, T, PIECE):
+                    h, n0 = divmod(c0, BANK)
+                    piece = old_t[j][:, c0 : c0 + PIECE]
+                    nc.vector.tensor_tensor(piece, piece, fade_ps[h][:, n0 : n0 + PIECE], ALU.mult)
+                for h in range(2):
+                    faded[j, h] = old_t[j][:, h * BANK : (h + 1) * BANK]
+
+        def values_gradient(js, copy, bank):
+            gv_ps = ps.tile([P, len(js), PAGE, G], F32, name="gv_ps%d" % js[0], tag=bank)
+            for n, j in enumerate(js):
+                gc, gs = g_parts[j // 2]
+                nc.tensor.matmul_mx(
+                    gv_ps[:, n].rearrange("p k g -> p (k g)"),
+                    lhsT=gc[:, j % 2 * P : (j % 2 + 1) * P].bitcast(FP8X4),
+                    lhsT_scale=gs[:, j % 2 * P : (j % 2 + 1) * P],
+                    rhs=wc[:].bitcast(FP8X4),
+                    rhs_scale=ws[:],
+                    start=True,
+                    stop=True,
+                )
+            gv = sb.tile([P, len(js), G, PAGE], F32, name="gv%d" % js[0])
+            copy(gv[:], gv_ps[:].rearrange("p n k g -> p n g k"))
+            return [gv[:, n].rearrange("p g k -> p (g k)") for n in range(len(js))]
+
+        (gv0,) = values_gradient([0], nc.scalar.copy, "b0")
         nc.scalar.activation(gf[0][:].indirect(offsets[:]), gv0, ACT.Copy)
-        gv1 = leave_psum(1, nc.vector.tensor_copy, "bg1")
-        gv2 = leave_psum(2, nc.vector.tensor_copy, "a1")
+        (gv1,) = values_gradient([1], nc.vector.tensor_copy, "b1")
+        (gv2,) = values_gradient([2], nc.vector.tensor_copy, "f0")
         nc.vector.tensor_copy(gf[1][:].indirect(offsets[:]), gv1)
-        gv3 = leave_psum(3, nc.scalar.copy, "bg0")
+        (gv3,) = values_gradient([3], nc.scalar.copy, "b0")
         nc.scalar.activation(gf[2][:].indirect(offsets[:]), gv2, ACT.Copy)
         nc.scalar.activation(gf[3][:].indirect(offsets[:]), gv3, ACT.Copy)
 
-        faded = [sb.tile([P, T], F32, name="faded0", tag="q1", align_bytes=64)] + old_t[1:3]
-        faded.append(sb.tile([P, T], F32, name="faded3"))
-        for j in range(4):
-            for c0 in range(0, T, GP_COLS):
-                cols = slice(c0, c0 + GP_COLS)
-                h, n0 = divmod(c0, BANK)
-                if c0 >= (1024, 768, 0, 0)[j]:
-                    piece = old_t[j][:, cols].rearrange("p (n c) -> p n c", c=PACK)
-                    fades = fade_ps[h][:, :, n0 // PACK : (n0 + GP_COLS) // PACK].rearrange("p c n -> p n c")
-                    nc.vector.tensor_tensor(faded[j][:, cols].rearrange("p (n c) -> p n c", c=PACK), piece, fades, ALU.mult)
-                else:
-                    nc.gpsimd.tensor_tensor(faded[j][:, cols], old_t[j][:, cols], fade_sb[:, h, n0 : n0 + GP_COLS], ALU.mult)
-
+        turn_back(1, ("b1", "f0"))
         for j in range(4):
             edges = [0, BANK, T] if j < 3 else [0, BANK, 3 * T // 4, T]
             for c0, c1 in zip(edges, edges[1:]):
-                cols = slice(c0, c1)
-                nc.vector.tensor_tensor(faded[j][:, cols], faded[j][:, cols], gf[j][:, cols], ALU.add)
-                nc.sync.dma_start(out[j * P : (j + 1) * P, cols], faded[j][:, cols])
+                h, n0 = divmod(c0, BANK)
+                nc.vector.tensor_tensor(old_t[j][:, c0:c1], faded[j, h][:, n0 : n0 + c1 - c0], gf[j][:, c0:c1], ALU.add)
+                nc.sync.dma_start(out[j * P : (j + 1) * P, c0:c1], old_t[j][:, c0:c1])

from contextlib import ExitStack

import concourse.mybir as mybir
from concourse.masks import make_identity

D, E, T, I, Q, G = 512, 512, 1024, 256, 512, 32
FLOPS = 2 * (2 * D * Q * I + Q * E * I)

F32 = mybir.dt.float32
BF16 = mybir.dt.bfloat16
I32 = mybir.dt.int32
U32 = mybir.dt.uint32
U16 = mybir.dt.uint16
U8 = mybir.dt.uint8
FP8X4 = mybir.dt.float8_e4m3fn_x4
FP4X4 = mybir.dt.float4_e2m1fn_x4
ALU = mybir.AluOpType
ACT = mybir.ActivationFunctionType
AX = mybir.AxisListType

P = 128
PACK = 4
PAGE = I // G
HS = I // 2
HG = G // 2
BANK = 512
BLOCKS = T // P
PIECE = 256
Q2_VECTOR = 88
Q1_VECTOR = 48
TURNED = (2, 3)


def tile_attend_bpagethensecond_v_kernel(
    tc, query, query2, keys_words, keys_scales, qs, grows, old, fade, offs, out
):
    nc = tc.nc
    with ExitStack() as ctx:
        sb = ctx.enter_context(tc.tile_pool(name="sb", bufs=1))
        ps = ctx.enter_context(tc.psum_pool(name="ps", bufs=1))

        offsets = sb.tile([P, I // 16], U16, name="offsets")
        key_words = sb.tile([P, T], U16, name="key_words")
        key_bytes = sb.tile([P, T], U8, name="key_bytes")
        fade_rows = sb.tile([P, P], F32, name="fade_rows")
        nc.gpsimd.memset(key_bytes[:].bitcast(I32), 0)
        nc.gpsimd.memset(fade_rows[:], 0.0)
        ident = sb.tile([P, P], F32, name="ident")
        make_identity(nc, ident[:])

        nc.sync.dma_start(offsets[:], offs)
        nc.sync.dma_start(key_words[:].bitcast(I32), keys_words[0].bitcast(I32))
        for u in range(4):
            nc.sync.dma_start(
                key_bytes[32 * u : 32 * u + 4, :].bitcast(I32), keys_scales[0, 4 * u : 4 * u + 4, :].bitcast(I32)
            )
        nc.sync.dma_start(fade_rows[0:BLOCKS, :], fade.rearrange("o (c n) -> (o c) n", n=P))
        q2_raw = sb.tile([P, PACK, Q], F32, name="q2_raw")
        nc.sync.dma_start(q2_raw[:], query2.rearrange("(p j) q -> p j q", j=PACK))
        q1_raw = sb.tile([P, PACK, Q], F32, name="q1_raw")
        nc.sync.dma_start(q1_raw[:], query.rearrange("(p j) q -> p j q", j=PACK))
        row_scale = sb.tile([P, PACK], F32, name="row_scale")
        nc.sync.dma_start(row_scale[:], qs.rearrange("(p j) o -> p (j o)", j=PACK))
        g_raw = sb.tile([P, PACK, E], F32, name="g_raw")
        old_t = [sb.tile([P, T], F32, name="old%d" % j) for j in range(4)]
        for n, j in enumerate((2, 3, 0, 1)):
            if n == 0:
                nc.sync.dma_start(g_raw[:], grows.rearrange("(p j) e -> p j e", j=PACK))
            nc.sync.dma_start(old_t[j][:], old[j * P : (j + 1) * P, :])

        gf = [sb.tile([P, T], F32, name="gf%d" % j) for j in range(4)]
        for j in range(4):
            nc.vector.memset(gf[j][:], 0.0)

        kw = sb.tile([P, I], U16, name="kw", align_bytes=64)
        kb = sb.tile([P, I], U8, name="kb", align_bytes=64)
        nc.vector.tensor_copy(kw[:], key_words[:].indirect(offsets[:]))

        def quantise(grouped, words, name):
            codes = sb.tile([P, words], U32, name=name + "_codes", align_bytes=64)
            scales = sb.tile([P, words], U8, name=name + "_scales", align_bytes=64)
            nc.vector.quantize_mx(out=codes[:].bitcast(FP8X4), scales=scales[:], in_=grouped)
            return codes, scales

        def deal(raw, name, split):
            grouped = sb.tile([P, PACK, P, PACK], BF16, name=name, align_bytes=64)
            dst = grouped[:].rearrange("p r m j -> p m j r")
            src = raw[:].rearrange("p j (m r) -> p m j r", r=PACK)
            nc.vector.tensor_copy(dst[:, :split], src[:, :split])
            nc.scalar.copy(dst[:, split:], src[:, split:])
            return grouped[:].rearrange("p r m j -> p (r m j)")

        def page_sums(tile, name):
            turned_ps = ps.tile([P, P], F32, name=name, tag=name)
            for k in range(PAGE):
                nc.tensor.matmul(
                    turned_ps[:],
                    lhsT=tile[:, k, :],
                    rhs=ident[:],
                    is_transpose=True,
                    start=(k == 0),
                    stop=(k == PAGE - 1),
                )
            return turned_ps

        q2_dealt = deal(q2_raw, "q2", Q2_VECTOR)
        nc.vector.tensor_copy(kb[:], key_bytes[:].indirect(offsets[:]))
        q2c, q2s = quantise(q2_dealt, Q, "q2")
        b_ps = [ps.tile([P, PACK, HS], F32, name="b_ps%d" % h, tag="b%d" % h) for h in range(2)]
        for h in range(2):
            for r in range(PACK):
                nc.tensor.matmul_mx(
                    b_ps[h][:, r, :],
                    lhsT=q2c[:, r * P : (r + 1) * P].bitcast(FP8X4),
                    lhsT_scale=q2s[:, r * P : (r + 1) * P],
                    rhs=kw[:, h * HS : (h + 1) * HS].bitcast(FP4X4),
                    rhs_scale=kb[:, h * HS : (h + 1) * HS],
                    start=True,
                    stop=True,
                )

        q1c, q1s = quantise(deal(q1_raw, "q1", Q1_VECTOR), Q, "q1")
        a_ps = [ps.tile([P, 2, I], F32, name="a_ps%d" % u, tag="a%d" % u) for u in range(2)]
        for r in range(PACK):
            nc.tensor.matmul_mx(
                a_ps[r // 2][:, r % 2, :],
                lhsT=q1c[:, r * P : (r + 1) * P].bitcast(FP8X4),
                lhsT_scale=q1s[:, r * P : (r + 1) * P],
                rhs=kw[:].bitcast(FP4X4),
                rhs_scale=kb[:],
                start=True,
                stop=True,
            )

        pb = sb.tile([P, PAGE, G * PACK], F32, name="pb")
        top = [sb.tile([P, HG, PACK], F32, name="top%d" % h) for h in range(2)]
        for h in range(2):
            nc.vector.tensor_reduce(
                top[h][:], b_ps[h][:].rearrange("p r (g k) -> p g r k", k=PAGE), axis=AX.X, op=ALU.max
            )
        for u in range(2):
            places = slice(u * PAGE // 2, (u + 1) * PAGE // 2)
            shifted = sb.tile([P, PAGE // 2, G, PACK], F32, name="shifted%d" % u, tag="sh%d" % u, align_bytes=64)
            for h in range(2):
                nc.vector.tensor_tensor(
                    shifted[:, :, h * HG : (h + 1) * HG, :],
                    b_ps[h][:].rearrange("p r (g k) -> p k g r", k=PAGE)[:, places],
                    top[h][:].unsqueeze(1).to_broadcast([P, PAGE // 2, HG, PACK]),
                    ALU.subtract,
                )
            nc.scalar.activation(
                pb[:, places, :].rearrange("p k c -> p (k c)"), shifted[:].rearrange("p k g r -> p (k g r)"), ACT.Exp
            )
        sb_t_ps = page_sums(pb, "sum_b")
        inv_t = sb.tile([P, P], F32, name="inv_t")
        nc.vector.reciprocal(inv_t[:], sb_t_ps[:])
        inv_ps = ps.tile([P, G, PACK], F32, name="inv_ps", tag="sum_b")
        nc.tensor.transpose(inv_ps[:].rearrange("p g r -> p (g r)"), inv_t[:], ident[:])

        pa = sb.tile([P, PACK, G, PAGE], F32, name="pa")
        sa = sb.tile([P, PACK, G], F32, name="sa")
        z = sb.tile([P, PACK], F32, name="z")
        for u in range(2):
            neg_top = sb.tile([P, 2], F32, name="neg_top%d" % u)
            nc.vector.tensor_reduce(neg_top[:], a_ps[u][:], axis=AX.X, op=ALU.max, negate=True)
            for v in range(2):
                r = 2 * u + v
                nc.scalar.activation(
                    pa[:, r].rearrange("p g k -> p (g k)"),
                    a_ps[u][:, v, :],
                    ACT.Exp,
                    bias=neg_top[:, v : v + 1],
                    accum_out=z[:, r : r + 1],
                )
        z_inv = sb.tile([P, PACK], F32, name="z_inv")
        nc.vector.reciprocal(z_inv[:], z[:])
        row_factor = sb.tile([P, PACK], F32, name="row_factor")
        nc.vector.tensor_tensor(row_factor[:], z_inv[:], row_scale[:], ALU.mult)
        for r in range(0, PACK, 1):
            nc.vector.tensor_reduce(sa[:, r : r + 1], pa[:, r : r + 1], axis=AX.X, op=ALU.add)
        share = sb.tile([P, G, PACK], F32, name="share")
        nc.vector.tensor_tensor(
            share[:], sa[:].rearrange("p r g -> p g r"), row_factor[:].unsqueeze(1).to_broadcast([P, G, PACK]), ALU.mult
        )
        factor = sb.tile([P, G, PACK], F32, name="factor")
        nc.vector.tensor_tensor(factor[:], inv_ps[:], share[:], ALU.mult)

        cols_ps = ps.tile([P, P], F32, name="cols_ps", tag="f1")
        nc.tensor.transpose(cols_ps[:], fade_rows[:], ident[:])
        fade_cols = sb.tile([P, BLOCKS], F32, name="fade_cols")
        nc.scalar.copy(fade_cols[:], cols_ps[:, 0:BLOCKS])
        fade_ps = [ps.tile([P, BANK], F32, name="fade_ps%d" % h, tag="f%d" % h) for h in range(2)]
        for c in range(BLOCKS):
            nc.tensor.transpose(
                fade_ps[c // 4][:, c % 4 * P : (c % 4 + 1) * P], fade_cols[:, c : c + 1].to_broadcast([P, P]), ident[:]
            )

        g_grouped = [
            sb.tile([P, E // 2, PACK], BF16, name="g_grouped%d" % h, align_bytes=64, tag=("g0", "sh1")[h]) for h in range(2)
        ]
        for v in range(4):
            nc.scalar.copy(
                g_grouped[v // 2][:, v % 2 * P : (v % 2 + 1) * P, :].rearrange("p (c i) j -> p c j i", i=4),
                g_raw[:, :, v * P : (v + 1) * P].rearrange("p j (c i) -> p c j i", i=4),
            )
        g_parts = [quantise(g_grouped[0][:].rearrange("p e j -> p (e j)"), E // 2, "g0")]

        wq = sb.tile([P, PAGE, G * PACK], BF16, name="wq", align_bytes=64)
        nc.vector.tensor_tensor(
            wq[:],
            pb[:],
            factor[:].rearrange("p g r -> p (g r)").unsqueeze(1).to_broadcast([P, PAGE, G * PACK]),
            ALU.mult,
        )
        wc, ws = quantise(wq[:].rearrange("p k c -> p (k c)"), I, "w")
        g_parts.append(quantise(g_grouped[1][:].rearrange("p e j -> p (e j)"), E // 2, "g1"))

        nt = len(TURNED)
        scaled = []
        for c0 in range(0, BLOCKS, 2):
            stage = ps.tile([P, 2, nt, P], F32, name="stage%d" % c0, tag="b%d" % (c0 // 2 % 2))
            for c in range(2):
                for n, j in enumerate(TURNED):
                    nc.tensor.transpose(stage[:, c, n, :], old_t[j][:, (c0 + c) * P : (c0 + c + 1) * P], ident[:])
            for c in range(2):
                block = sb.tile([P, nt, P], F32, name="scaled%d" % (c0 + c))
                nc.scalar.activation(block[:], stage[:, c], ACT.Copy, scale=fade_cols[:, c0 + c : c0 + c + 1])
                scaled.append(block)
        faded = {}

        def turn_back(n, banks):
            for h in range(2):
                back = ps.tile([P, BANK], F32, name="back%d%d" % (n, h), tag=banks[h])
                for c in range(4):
                    nc.tensor.transpose(back[:, c * P : (c + 1) * P], scaled[4 * h + c][:, n, :], ident[:])
                faded[TURNED[n], h] = back

        turn_back(0, ("a0", "a1"))
        for j in range(4):
            if j not in TURNED:
                for c0 in range(0, T, PIECE):
                    h, n0 = divmod(c0, BANK)
                    piece = old_t[j][:, c0 : c0 + PIECE]
                    nc.vector.tensor_tensor(piece, piece, fade_ps[h][:, n0 : n0 + PIECE], ALU.mult)
                for h in range(2):
                    faded[j, h] = old_t[j][:, h * BANK : (h + 1) * BANK]

        def values_gradient(js, copy, bank):
            gv_ps = ps.tile([P, len(js), PAGE, G], F32, name="gv_ps%d" % js[0], tag=bank)
            for n, j in enumerate(js):
                gc, gs = g_parts[j // 2]
                nc.tensor.matmul_mx(
                    gv_ps[:, n].rearrange("p k g -> p (k g)"),
                    lhsT=gc[:, j % 2 * P : (j % 2 + 1) * P].bitcast(FP8X4),
                    lhsT_scale=gs[:, j % 2 * P : (j % 2 + 1) * P],
                    rhs=wc[:].bitcast(FP8X4),
                    rhs_scale=ws[:],
                    start=True,
                    stop=True,
                )
            gv = sb.tile([P, len(js), G, PAGE], F32, name="gv%d" % js[0])
            copy(gv[:], gv_ps[:].rearrange("p n k g -> p n g k"))
            return [gv[:, n].rearrange("p g k -> p (g k)") for n in range(len(js))]

        (gv0,) = values_gradient([0], nc.scalar.copy, "b0")
        nc.scalar.activation(gf[0][:].indirect(offsets[:]), gv0, ACT.Copy)
        (gv1,) = values_gradient([1], nc.vector.tensor_copy, "b1")
        (gv2,) = values_gradient([2], nc.vector.tensor_copy, "f0")
        nc.vector.tensor_copy(gf[1][:].indirect(offsets[:]), gv1)
        (gv3,) = values_gradient([3], nc.scalar.copy, "b0")
        nc.scalar.activation(gf[2][:].indirect(offsets[:]), gv2, ACT.Copy)
        nc.scalar.activation(gf[3][:].indirect(offsets[:]), gv3, ACT.Copy)

        turn_back(1, ("b1", "f0"))
        for j in range(4):
            edges = [0, BANK, T] if j < 3 else [0, BANK, 3 * T // 4, T]
            for c0, c1 in zip(edges, edges[1:]):
                h, n0 = divmod(c0, BANK)
                nc.vector.tensor_tensor(old_t[j][:, c0:c1], faded[j, h][:, n0 : n0 + c1 - c0], gf[j][:, c0:c1], ALU.add)
                nc.sync.dma_start(out[j * P : (j + 1) * P, c0:c1], old_t[j][:, c0:c1])
